import numpy as np
import ml_dtypes


def mxq(x, axis, fmt="e4m3"):
    dtype, down = {"e4m3": (ml_dtypes.float8_e4m3fn, 7), "e5m2": (ml_dtypes.float8_e5m2, 14)}[fmt]
    v = np.moveaxis(np.asarray(x, np.float32).astype(ml_dtypes.bfloat16).astype(np.float64), axis, -1)
    blocks = v.reshape(v.shape[:-1] + (-1, 32))
    amax = np.abs(blocks).max(-1, keepdims=True)
    byte = np.maximum(np.where(amax > 0, np.frexp(amax)[1] - 1 + 127, 0) - down, 1)
    scale = np.exp2(byte - 127.0)
    codes = (blocks / scale).astype(np.float32).astype(dtype).astype(np.float64)
    return np.moveaxis((codes * scale).reshape(v.shape), -1, axis)


WIDE = False


def mx_kscale(k):
    if not WIDE:
        return np.ones(k)
    levels = np.array([10, -10, 5, -5, 0])
    if k % 512:
        return np.exp2(np.random.permutation(np.resize(levels, k // 32))).repeat(32)
    a = np.empty((k // 512, 16))
    for p in range(k // 512):
        a[p, :8] = np.random.permutation(np.resize(levels, 8))
        for g in range(8):
            far = levels[np.abs(levels - a[p, g]) >= 10]
            a[p, g + 8] = far[np.random.randint(len(far))]
    return np.exp2(a.ravel()).repeat(32)


def f64(x):
    return np.asarray(x).astype(np.float64)


def striped(idx):
    return np.tile(idx.reshape(-1, 16).T, (8, 1)).astype(np.uint16)


def unstriped(offs):
    return offs[:16].T.reshape(-1).astype(np.int64)


K, T, E, C, N = 512, 768, 24, 128, 128
TOP = 4


def by_expert(wq, xq):
    return np.concatenate([wq[e].T @ xq[:, e * C:(e + 1) * C] for e in range(E)], axis=1)


def setup_inputs():
    n = np.random.standard_normal
    s = mx_kscale(K)[:, None]
    deal = np.repeat(np.arange(E), C).reshape(TOP, T)[:, np.random.permutation(T)]
    deal = np.take_along_axis(deal, np.argsort(np.random.rand(TOP, T), axis=0), axis=0)
    for _ in range(8):
        s_, t_ = np.random.permutation(T).reshape(2, -1); r = np.random.randint(TOP, size=T // 2); x, y = deal[r, s_].copy(), deal[r, t_].copy()
        ok = ~((deal[:, s_] == y).any(0) | (deal[:, t_] == x).any(0)); deal[r[ok], s_[ok]] = y[ok]; deal[r[ok], t_[ok]] = x[ok]
    order = np.lexsort((np.random.rand(TOP * T), deal.reshape(-1)))
    slot_token = order % T; pos = np.empty(TOP * T, np.int64); pos[order] = np.arange(TOP * T); pos = pos.reshape(TOP, T)
    g = np.random.uniform(0.5, 1.5, (TOP, T)); g = g / g.sum(0)
    w_slot = np.empty(E * C)
    for r in range(TOP): w_slot[pos[r]] = g[r]
    return {
        "xT": (n((K, T)) * s).astype(np.float32),
        "w": (n((E, K, N)) / np.sqrt(K) / s[None]).astype(np.float32),
        "gate": np.tile(w_slot, (K, 1)).astype(np.float32),
        "offs": striped(slot_token),
        "pos1": striped(pos[0]),
        "pos2": striped(pos[1]),
        "pos3": striped(pos[2]),
        "pos4": striped(pos[3]),
    }


def reference(xT, w, gate, offs, pos1, pos2, pos3, pos4):
    idx = unstriped(offs)
    xq = mxq(f64(gate) * f64(xT)[:, idx], 0, "e4m3")
    y = by_expert(mxq(f64(w), 1, "e4m3"), xq)
    return y[:, unstriped(pos1)] + y[:, unstriped(pos2)] + y[:, unstriped(pos3)] + y[:, unstriped(pos4)]

@@ -1,0 +1,156 @@
+from contextlib import ExitStack
+
+import concourse.mybir as mybir
+
+K, T, E, C, N = 512, 768, 24, 128, 128
+TOP = 4
+S = E * C
+
+FLOPS = 2 * K * N * S
+BYTES = 4 * (K * T + E * K * N + S + N * T) + 2 * 128 * (S + TOP * T) // 16
+
+F32 = mybir.dt.float32
+BF16 = mybir.dt.bfloat16
+U32 = mybir.dt.uint32
+U16 = mybir.dt.uint16
+U8 = mybir.dt.uint8
+FP8X4 = mybir.dt.float8_e4m3fn_x4
+MULT = mybir.AluOpType.mult
+ADD = mybir.AluOpType.add
+
+P = 128
+PACK = 4
+GROUP = 4
+WIDE = GROUP * C
+GROUPS = E // GROUP
+LAST = [256,128,128]
+HALF = T // 2
+
+
+def tile_moe_pre_lin_none_kernel(tc, xT, w, gate, offs, pos1, pos2, pos3, pos4, out):
+    nc = tc.nc
+    with ExitStack() as ctx:
+        keep = ctx.enter_context(tc.tile_pool(name="keep", bufs=1))
+        ring = ctx.enter_context(tc.tile_pool(name="ring", bufs=2))
+        psum = ctx.enter_context(tc.psum_pool(name="psum", bufs=1))
+
+        offsets = keep.tile([P, S // 16], U16, name="offsets")
+        back = [keep.tile([P, T // 16], U16, name="back%d" % r) for r in range(TOP)]
+        tokens = [keep.tile([P, T], F32, name="tokens%d" % t) for t in range(PACK)]
+        gates = [keep.tile([P, WIDE], F32, name="gates%d" % g) for g in range(GROUPS)]
+        w_raw = [keep.tile([P, GROUP, PACK, N], F32, name="w_raw%d" % g) for g in range(GROUPS)]
+        w_round = [keep.tile([P, GROUP * N * PACK], BF16, name="w_round%d" % g, align_bytes=64) for g in range(GROUPS)]
+        w_codes = [keep.tile([P, GROUP * N], U32, name="w_codes%d" % g, align_bytes=64) for g in range(GROUPS)]
+        w_scales = [keep.tile([P, GROUP * N], U8, name="w_scales%d" % g, align_bytes=64) for g in range(GROUPS)]
+        y = keep.tile([P, S], F32, name="y")
+
+        widths = [WIDE] * (GROUPS - 1) + LAST
+        starts = [sum(widths[:c]) for c in range(len(widths))]
+        chunks = len(widths)
+        x_round = [keep.tile([P, widths[c] * PACK], BF16, name="x_round%d" % c, align_bytes=64) for c in range(chunks)]
+        x_codes = [keep.tile([P, widths[c]], U32, name="x_codes%d" % c, align_bytes=64) for c in range(chunks)]
+        x_scales = [keep.tile([P, widths[c]], U8, name="x_scales%d" % c, align_bytes=64) for c in range(chunks)]
+        sums = [psum.tile([P, widths[c]], F32, name="sums%d" % c) for c in range(chunks)]
+
+        x_rows = xT.rearrange("(p t) j -> p t j", t=PACK)
+
+        def load_gate(g):
+            nc.sync.dma_start(gates[g][:], gate[0:P, g * WIDE:(g + 1) * WIDE])
+
+        def load_w(g):
+            nc.sync.dma_start(
+                w_raw[g][:].rearrange("p e t n -> p e (t n)"),
+                w[g * GROUP:(g + 1) * GROUP].rearrange("e (p t) n -> p e (t n)", t=PACK),
+            )
+
+        nc.sync.dma_start(offsets[:], offs)
+        nc.sync.dma_start(tokens[0][:], x_rows[:, 0, :])
+        load_gate(0)
+        for t in range(1, PACK):
+            nc.sync.dma_start(tokens[t][:], x_rows[:, t, :])
+        for g in range(GROUPS):
+            if g + 1 < GROUPS:
+                load_gate(g + 1)
+            load_w(g)
+        for r, pos in enumerate((pos1, pos2, pos3, pos4)):
+            nc.sync.dma_start(back[r][:], pos)
+
+        def gather(c):
+            s0, n = starts[c], widths[c]
+            g, g0 = divmod(s0, WIDE)
+            tile = ring.tile([P, PACK, n], F32, name="picked")
+            for t in range(PACK):
+                nc.vector.tensor_tensor(
+                    tile[:, t, :],
+                    tokens[t][:].indirect(offsets[:, s0 // 16:(s0 + n) // 16]),
+                    gates[g][:, g0:g0 + n],
+                    MULT,
+                )
+            return tile
+
+        def round_x(c, tile):
+            nc.scalar.copy(
+                x_round[c][:].rearrange("p (c i t) -> p c t i", i=2, t=PACK),
+                tile[:].rearrange("p t (c i) -> p c t i", i=2),
+            )
+
+        def round_w(g):
+            nc.scalar.copy(
+                w_round[g][:].rearrange("p (e c i t) -> p e c t i", e=GROUP, i=2, t=PACK),
+                w_raw[g][:].rearrange("p e t (c i) -> p e c t i", i=2),
+            )
+
+        def quantize_x(c):
+            nc.vector.quantize_mx(out=x_codes[c][:].bitcast(FP8X4), scales=x_scales[c][:], in_=x_round[c][:])
+
+        def quantize_w(g):
+            nc.vector.quantize_mx(out=w_codes[g][:].bitcast(FP8X4), scales=w_scales[g][:], in_=w_round[g][:])
+
+        def multiply(c):
+            for j in range(widths[c] // C):
+                g, e = divmod(starts[c] // C + j, GROUP)
+                cols = slice(j * C, (j + 1) * C)
+                outs = slice(e * N, (e + 1) * N)
+                nc.tensor.matmul_mx(
+                    out=sums[c][:, cols],
+                    lhsT=w_codes[g][:, outs].bitcast(FP8X4),
+                    lhsT_scale=w_scales[g][:, outs],
+                    rhs=x_codes[c][:, cols].bitcast(FP8X4),
+                    rhs_scale=x_scales[c][:, cols],
+                    start=True,
+                    stop=True,
+                )
+
+        def empty(c):
+            nc.scalar.copy(y[:, starts[c]:starts[c] + widths[c]], sums[c][:])
+
+        tiles_list = [gather(0)]
+        for c in range(chunks):
+            if c + 1 < chunks:
+                tiles_list.append(gather(c + 1))
+            round_x(c, tiles_list[c])
+            if c == 0:
+                round_w(0)
+                quantize_w(0)
+            if c + 1 < GROUPS:
+                round_w(c + 1)
+            quantize_x(c)
+            if c + 1 < GROUPS:
+                quantize_w(c + 1)
+            multiply(c)
+            if c >= 1:
+                empty(c - 1)
+        empty(chunks - 1)
+
+        parts = []
+        for r in range(TOP):
+            for h in range(2):
+                window = y[:].indirect(back[r][:, h * HALF // 16:(h + 1) * HALF // 16])
+                total = keep.tile([P, HALF], F32, name="total%d_%d" % (r, h))
+                if r == 0:
+                    nc.vector.tensor_copy(total[:], window)
+                else:
+                    nc.vector.tensor_tensor(total[:], window, parts[-2][:], ADD)
+                parts.append(total)
+                if r == TOP - 1:
+                    nc.sync.dma_start(out[:, h * HALF:(h + 1) * HALF], total[:])

@@ -20,99 +20,123 @@ ADD = mybir.AluOpType.add
 
 P = 128
 PACK = 4
-GROUP = 4
-WIDE = GROUP * C
-GROUPS = E // GROUP
-LAST = [256,128,128]
-HALF = T // 2
+BANK = 512
+WINDOW = 1152
+WIDTHS = [512,1024,1024,384,128]
+W_GROUPS = [4,2,2,4,4,4,4]
+GATE_CUTS = [0,128,512,1024,1536,2560,3072]
+FIRST_CUTS = [[0,128,512],[0,512,1024],[0,1024],[0,384],[0,128]]
+LOADS = ["o0","x0","g0","g1","x1","x2","x3","w1","g2","g3","w2","w4","w0","g4","w5","g5","w6","w3","p0","p1","p2","p3"]
+STEPS = ["G0","G1","W1","X0","Q00","W2","W4","W0","R0","M00","G2","X1","Q10","W5","R2","W6","R3","W3","R1","M10","E00","G3","X2","Q20","M20","G4","Q21","M21","E10","E11","X3","Q30","M30","Q31","M31","X4","Q40","M40","E20","E21","e30","e40"]
+REUSE = ["w_raw1","w_raw0","w_raw3","x3","x4"]
+W_SETS = [4,8,8,4]
+PICKED = ["pa","pb","pa","w_round1","pa"]
+Q_CUTS = [[0,512],[0,1024],[0,512,1024],[0,256,384],[0,128]]
+OUT_CUTS = [[0,384,768],[0,384,768],[0,384,768],[0,384,640,768]]
 
 
 def tile_moe_pre_lin_none_kernel(tc, xT, w, gate, offs, pos1, pos2, pos3, pos4, out):
     nc = tc.nc
     with ExitStack() as ctx:
         keep = ctx.enter_context(tc.tile_pool(name="keep", bufs=1))
-        ring = ctx.enter_context(tc.tile_pool(name="ring", bufs=2))
         psum = ctx.enter_context(tc.psum_pool(name="psum", bufs=1))
+
+        groups = len(W_GROUPS)
+        e0 = [sum(W_GROUPS[:g]) for g in range(groups)]
+        owner = [(q, j) for q in range(len(W_SETS)) for j in range(W_SETS[q])]
+        chunks = len(WIDTHS)
+        starts = [sum(WIDTHS[:c]) for c in range(chunks)]
 
         offsets = keep.tile([P, S // 16], U16, name="offsets")
         back = [keep.tile([P, T // 16], U16, name="back%d" % r) for r in range(TOP)]
-        tokens = [keep.tile([P, T], F32, name="tokens%d" % t) for t in range(PACK)]
-        gates = [keep.tile([P, WIDE], F32, name="gates%d" % g) for g in range(GROUPS)]
-        w_raw = [keep.tile([P, GROUP, PACK, N], F32, name="w_raw%d" % g) for g in range(GROUPS)]
-        w_round = [keep.tile([P, GROUP * N * PACK], BF16, name="w_round%d" % g, align_bytes=64) for g in range(GROUPS)]
-        w_codes = [keep.tile([P, GROUP * N], U32, name="w_codes%d" % g, align_bytes=64) for g in range(GROUPS)]
-        w_scales = [keep.tile([P, GROUP * N], U8, name="w_scales%d" % g, align_bytes=64) for g in range(GROUPS)]
+        tokens = [keep.tile([P, WINDOW], F32, name="tokens%d" % t) for t in range(PACK)]
+        gates = keep.tile([P, S], F32, name="gates")
+        w_raw = [keep.tile([P, W_GROUPS[g], PACK, N], F32, name="w_raw%d" % g, tag="w_raw%d" % g, align_bytes=64) for g in range(groups)]
+        w_round = [keep.tile([P, n * N * PACK], BF16, name="w_round%d" % q, tag="w_round%d" % q, align_bytes=64) for q, n in enumerate(W_SETS)]
+        w_codes = [keep.tile([P, n * N], U32, name="w_codes%d" % q, align_bytes=64) for q, n in enumerate(W_SETS)]
+        w_scales = [keep.tile([P, n * N], U8, name="w_scales%d" % q, align_bytes=64) for q, n in enumerate(W_SETS)]
         y = keep.tile([P, S], F32, name="y")
-
-        widths = [WIDE] * (GROUPS - 1) + LAST
-        starts = [sum(widths[:c]) for c in range(len(widths))]
-        chunks = len(widths)
-        x_round = [keep.tile([P, widths[c] * PACK], BF16, name="x_round%d" % c, align_bytes=64) for c in range(chunks)]
-        x_codes = [keep.tile([P, widths[c]], U32, name="x_codes%d" % c, align_bytes=64) for c in range(chunks)]
-        x_scales = [keep.tile([P, widths[c]], U8, name="x_scales%d" % c, align_bytes=64) for c in range(chunks)]
-        sums = [psum.tile([P, widths[c]], F32, name="sums%d" % c) for c in range(chunks)]
+        x_round = {}
+        x_codes = [keep.tile([P, WIDTHS[c]], U32, name="x_codes%d" % c, align_bytes=64) for c in range(chunks)]
+        x_scales = [keep.tile([P, WIDTHS[c]], U8, name="x_scales%d" % c, align_bytes=64) for c in range(chunks)]
+        sums = [
+            [psum.tile([P, min(BANK, WIDTHS[c] - b)], F32, name="sums%d_%d" % (c, b)) for b in range(0, WIDTHS[c], BANK)]
+            for c in range(chunks)
+        ]
 
         x_rows = xT.rearrange("(p t) j -> p t j", t=PACK)
 
-        def load_gate(g):
-            nc.sync.dma_start(gates[g][:], gate[0:P, g * WIDE:(g + 1) * WIDE])
+        def load(kind, n):
+            if kind == "o":
+                nc.sync.dma_start(offsets[:], offs)
+            if kind == "x":
+                nc.sync.dma_start(tokens[n][:, 0:T], x_rows[:, n, :])
+            if kind == "g":
+                nc.sync.dma_start(gates[:, GATE_CUTS[n]:GATE_CUTS[n + 1]], gate[0:P, GATE_CUTS[n]:GATE_CUTS[n + 1]])
+            if kind == "w":
+                nc.sync.dma_start(
+                    w_raw[n][:].rearrange("p e t n -> p e (t n)"),
+                    w[e0[n]:e0[n] + W_GROUPS[n]].rearrange("e (p t) n -> p e (t n)", t=PACK),
+                )
+            if kind == "p":
+                nc.sync.dma_start(back[n][:], (pos1, pos2, pos3, pos4)[n])
 
-        def load_w(g):
-            nc.sync.dma_start(
-                w_raw[g][:].rearrange("p e t n -> p e (t n)"),
-                w[g * GROUP:(g + 1) * GROUP].rearrange("e (p t) n -> p e (t n)", t=PACK),
-            )
+        for item in LOADS:
+            load(item[0], int(item[1:]))
 
-        nc.sync.dma_start(offsets[:], offs)
-        nc.sync.dma_start(tokens[0][:], x_rows[:, 0, :])
-        load_gate(0)
-        for t in range(1, PACK):
-            nc.sync.dma_start(tokens[t][:], x_rows[:, t, :])
-        for g in range(GROUPS):
-            if g + 1 < GROUPS:
-                load_gate(g + 1)
-            load_w(g)
-        for r, pos in enumerate((pos1, pos2, pos3, pos4)):
-            nc.sync.dma_start(back[r][:], pos)
+        picked = []
 
         def gather(c):
-            s0, n = starts[c], widths[c]
-            g, g0 = divmod(s0, WIDE)
-            tile = ring.tile([P, PACK, n], F32, name="picked")
+            s0, n = starts[c], WIDTHS[c]
+            tile = keep.tile([P, PACK, n], F32, name="picked%d" % c, tag=PICKED[c], align_bytes=64)
+            picked.append(tile)
             for t in range(PACK):
-                nc.vector.tensor_tensor(
-                    tile[:, t, :],
-                    tokens[t][:].indirect(offsets[:, s0 // 16:(s0 + n) // 16]),
-                    gates[g][:, g0:g0 + n],
-                    MULT,
-                )
-            return tile
+                cuts = FIRST_CUTS[c] if t == 0 else [0, n]
+                for a, b in zip(cuts[:-1], cuts[1:]):
+                    nc.vector.tensor_tensor(
+                        tile[:, t, a:b],
+                        tokens[t][:].indirect(offsets[:, (s0 + a) // 16:(s0 + b) // 16]),
+                        gates[:, s0 + a:s0 + b],
+                        MULT,
+                    )
 
-        def round_x(c, tile):
-            nc.scalar.copy(
+        def mover(on_vector):
+            return nc.vector.tensor_copy if on_vector else nc.scalar.copy
+
+        def round_x(c, on_vector):
+            tile = keep.tile([P, WIDTHS[c] * PACK], BF16, name="x_round%d" % c, tag=REUSE[c], align_bytes=64)
+            x_round.setdefault(c, tile)
+            mover(on_vector)(
                 x_round[c][:].rearrange("p (c i t) -> p c t i", i=2, t=PACK),
-                tile[:].rearrange("p t (c i) -> p c t i", i=2),
+                picked[c][:].rearrange("p t (c i) -> p c t i", i=2),
             )
 
-        def round_w(g):
-            nc.scalar.copy(
-                w_round[g][:].rearrange("p (e c i t) -> p e c t i", e=GROUP, i=2, t=PACK),
+        def round_w(g, on_vector):
+            q, j = owner[e0[g]]
+            mover(on_vector)(
+                w_round[q][:, j * N * PACK:(j + W_GROUPS[g]) * N * PACK].rearrange("p (e c i t) -> p e c t i", e=W_GROUPS[g], i=2, t=PACK),
                 w_raw[g][:].rearrange("p e t (c i) -> p e c t i", i=2),
             )
 
-        def quantize_x(c):
-            nc.vector.quantize_mx(out=x_codes[c][:].bitcast(FP8X4), scales=x_scales[c][:], in_=x_round[c][:])
+        def quantize_x(c, j):
+            a, b = Q_CUTS[c][j], Q_CUTS[c][j + 1]
+            nc.vector.quantize_mx(
+                out=x_codes[c][:, a:b].bitcast(FP8X4),
+                scales=x_scales[c][:, a:b],
+                in_=x_round[c][:, a * PACK:b * PACK],
+            )
 
         def quantize_w(g):
             nc.vector.quantize_mx(out=w_codes[g][:].bitcast(FP8X4), scales=w_scales[g][:], in_=w_round[g][:])
 
-        def multiply(c):
-            for j in range(widths[c] // C):
-                g, e = divmod(starts[c] // C + j, GROUP)
+        def multiply(c, piece):
+            for j in range(Q_CUTS[c][piece] // C, Q_CUTS[c][piece + 1] // C):
+                g, e = owner[starts[c] // C + j]
+                b, b0 = divmod(j * C, BANK)
                 cols = slice(j * C, (j + 1) * C)
                 outs = slice(e * N, (e + 1) * N)
                 nc.tensor.matmul_mx(
-                    out=sums[c][:, cols],
+                    out=sums[c][b][:, b0:b0 + C],
                     lhsT=w_codes[g][:, outs].bitcast(FP8X4),
                     lhsT_scale=w_scales[g][:, outs],
                     rhs=x_codes[c][:, cols].bitcast(FP8X4),
@@ -121,36 +145,38 @@ def tile_moe_pre_lin_none_kernel(tc, xT, w, gate, offs, pos1, pos2, pos3, pos4, 
                     stop=True,
                 )
 
-        def empty(c):
-            nc.scalar.copy(y[:, starts[c]:starts[c] + widths[c]], sums[c][:])
+        def empty(c, b, on_vector):
+            bank = sums[c][b]
+            s0 = starts[c] + b * BANK
+            mover(on_vector)(y[:, s0:s0 + bank.shape[1]], bank[:])
 
-        tiles_list = [gather(0)]
-        for c in range(chunks):
-            if c + 1 < chunks:
-                tiles_list.append(gather(c + 1))
-            round_x(c, tiles_list[c])
-            if c == 0:
-                round_w(0)
-                quantize_w(0)
-            if c + 1 < GROUPS:
-                round_w(c + 1)
-            quantize_x(c)
-            if c + 1 < GROUPS:
-                quantize_w(c + 1)
-            multiply(c)
-            if c >= 1:
-                empty(c - 1)
-        empty(chunks - 1)
+        for item in STEPS:
+            kind, n = item[0], int(item[1])
+            if kind == "G":
+                gather(n)
+            if kind in "Xx":
+                round_x(n, kind == "x")
+            if kind in "Ww":
+                round_w(n, kind == "w")
+            if kind == "Q":
+                quantize_x(n, int(item[2]))
+            if kind == "R":
+                quantize_w(n)
+            if kind == "M":
+                multiply(n, int(item[2]))
+            if kind in "Ee":
+                empty(n, int(item[2]), kind == "e")
 
-        parts = []
+        last = []
         for r in range(TOP):
-            for h in range(2):
-                window = y[:].indirect(back[r][:, h * HALF // 16:(h + 1) * HALF // 16])
-                total = keep.tile([P, HALF], F32, name="total%d_%d" % (r, h))
+            cuts = OUT_CUTS[r]
+            total = keep.tile([P, T], F32, name="total%d" % r)
+            for a, b in zip(cuts[:-1], cuts[1:]):
+                window = y[:].indirect(back[r][:, a // 16:b // 16])
                 if r == 0:
-                    nc.vector.tensor_copy(total[:], window)
+                    nc.vector.tensor_copy(total[:, a:b], window)
                 else:
-                    nc.vector.tensor_tensor(total[:], window, parts[-2][:], ADD)
-                parts.append(total)
+                    nc.vector.tensor_tensor(total[:, a:b], window, last[-1][:, a:b], ADD)
                 if r == TOP - 1:
-                    nc.sync.dma_start(out[:, h * HALF:(h + 1) * HALF], total[:])
+                    nc.sync.dma_start(out[:, a:b], total[:, a:b])
+            last.append(total)

@@ -20,163 +20,201 @@ ADD = mybir.AluOpType.add
 
 P = 128
 PACK = 4
+PER_COLUMN = 16
 BANK = 512
+RUN = 2
+
+CHUNKS = (512, 1024, 1024, 384, 128)
 WINDOW = 1152
-WIDTHS = [512,1024,1024,384,128]
-W_GROUPS = [4,2,2,4,4,4,4]
-GATE_CUTS = [0,128,512,1024,1536,2560,3072]
-FIRST_CUTS = [[0,128,512],[0,512,1024],[0,1024],[0,384],[0,128]]
-LOADS = ["o0","x0","g0","g1","x1","x2","x3","w1","g2","g3","w2","w4","w0","g4","w5","g5","w6","w3","p0","p1","p2","p3"]
-STEPS = ["G0","G1","W1","X0","Q00","W2","W4","W0","R0","M00","G2","X1","Q10","W5","R2","W6","R3","W3","R1","M10","E00","G3","X2","Q20","M20","G4","Q21","M21","E10","E11","X3","Q30","M30","Q31","M31","X4","Q40","M40","E20","E21","e30","e40"]
-REUSE = ["w_raw1","w_raw0","w_raw3","x3","x4"]
-W_SETS = [4,8,8,4]
-PICKED = ["pa","pb","pa","w_round1","pa"]
-Q_CUTS = [[0,512],[0,1024],[0,512,1024],[0,256,384],[0,128]]
-OUT_CUTS = [[0,384,768],[0,384,768],[0,384,768],[0,384,640,768]]
+W_LOADS = (4, 2, 2, 4, 4, 4, 4)
+W_SETS = (4, 8, 8, 4)
+EARLY = (128, 512)
+HALVES = (0, 384, 768)
+LAST_CUTS = (0, 384, 640, 768)
+
+
+def offsets_of(sizes):
+    return [sum(sizes[:i]) for i in range(len(sizes))]
 
 
 def tile_moe_pre_lin_none_kernel(tc, xT, w, gate, offs, pos1, pos2, pos3, pos4, out):
     nc = tc.nc
+    slot0 = offsets_of(CHUNKS)
+    expert0 = offsets_of(W_LOADS)
+    place = [(q, j) for q, n in enumerate(W_SETS) for j in range(n)]
+
     with ExitStack() as ctx:
         keep = ctx.enter_context(tc.tile_pool(name="keep", bufs=1))
         psum = ctx.enter_context(tc.psum_pool(name="psum", bufs=1))
 
-        groups = len(W_GROUPS)
-        e0 = [sum(W_GROUPS[:g]) for g in range(groups)]
-        owner = [(q, j) for q in range(len(W_SETS)) for j in range(W_SETS[q])]
-        chunks = len(WIDTHS)
-        starts = [sum(WIDTHS[:c]) for c in range(chunks)]
-
-        offsets = keep.tile([P, S // 16], U16, name="offsets")
-        back = [keep.tile([P, T // 16], U16, name="back%d" % r) for r in range(TOP)]
-        tokens = [keep.tile([P, WINDOW], F32, name="tokens%d" % t) for t in range(PACK)]
+        slot_tokens = keep.tile([P, S // PER_COLUMN], U16, name="slot_tokens")
+        token_slots = [keep.tile([P, T // PER_COLUMN], U16, name="token_slots%d" % r) for r in range(TOP)]
+        planes = [keep.tile([P, WINDOW], F32, name="plane%d" % t) for t in range(PACK)]
         gates = keep.tile([P, S], F32, name="gates")
-        w_raw = [keep.tile([P, W_GROUPS[g], PACK, N], F32, name="w_raw%d" % g, tag="w_raw%d" % g, align_bytes=64) for g in range(groups)]
-        w_round = [keep.tile([P, n * N * PACK], BF16, name="w_round%d" % q, tag="w_round%d" % q, align_bytes=64) for q, n in enumerate(W_SETS)]
+        w_raw = [
+            keep.tile([P, n, PACK, N], F32, name="w_raw%d" % g, tag="w_raw%d" % g, align_bytes=64)
+            for g, n in enumerate(W_LOADS)
+        ]
+        w_round = [
+            keep.tile([P, n * N * PACK], BF16, name="w_round%d" % q, tag="w_round%d" % q, align_bytes=64)
+            for q, n in enumerate(W_SETS)
+        ]
         w_codes = [keep.tile([P, n * N], U32, name="w_codes%d" % q, align_bytes=64) for q, n in enumerate(W_SETS)]
         w_scales = [keep.tile([P, n * N], U8, name="w_scales%d" % q, align_bytes=64) for q, n in enumerate(W_SETS)]
         y = keep.tile([P, S], F32, name="y")
-        x_round = {}
-        x_codes = [keep.tile([P, WIDTHS[c]], U32, name="x_codes%d" % c, align_bytes=64) for c in range(chunks)]
-        x_scales = [keep.tile([P, WIDTHS[c]], U8, name="x_scales%d" % c, align_bytes=64) for c in range(chunks)]
-        sums = [
-            [psum.tile([P, min(BANK, WIDTHS[c] - b)], F32, name="sums%d_%d" % (c, b)) for b in range(0, WIDTHS[c], BANK)]
-            for c in range(chunks)
+        x_codes = [keep.tile([P, n], U32, name="x_codes%d" % c, align_bytes=64) for c, n in enumerate(CHUNKS)]
+        x_scales = [keep.tile([P, n], U8, name="x_scales%d" % c, align_bytes=64) for c, n in enumerate(CHUNKS)]
+        banks = [
+            [psum.tile([P, min(BANK, n - b)], F32, name="bank%d_%d" % (c, b)) for b in range(0, n, BANK)]
+            for c, n in enumerate(CHUNKS)
         ]
 
         x_rows = xT.rearrange("(p t) j -> p t j", t=PACK)
 
-        def load(kind, n):
-            if kind == "o":
-                nc.sync.dma_start(offsets[:], offs)
-            if kind == "x":
-                nc.sync.dma_start(tokens[n][:, 0:T], x_rows[:, n, :])
-            if kind == "g":
-                nc.sync.dma_start(gates[:, GATE_CUTS[n]:GATE_CUTS[n + 1]], gate[0:P, GATE_CUTS[n]:GATE_CUTS[n + 1]])
-            if kind == "w":
-                nc.sync.dma_start(
-                    w_raw[n][:].rearrange("p e t n -> p e (t n)"),
-                    w[e0[n]:e0[n] + W_GROUPS[n]].rearrange("e (p t) n -> p e (t n)", t=PACK),
-                )
-            if kind == "p":
-                nc.sync.dma_start(back[n][:], (pos1, pos2, pos3, pos4)[n])
+        def load_plane(t):
+            nc.sync.dma_start(planes[t][:, 0:T], x_rows[:, t, :])
 
-        for item in LOADS:
-            load(item[0], int(item[1:]))
+        def load_gate(a, b):
+            nc.sync.dma_start(gates[:, a:b], gate[0:P, a:b])
 
-        picked = []
+        def load_w(g):
+            nc.sync.dma_start(
+                w_raw[g][:].rearrange("p e t n -> p e (t n)"),
+                w[expert0[g]:expert0[g] + W_LOADS[g]].rearrange("e (p t) n -> p e (t n)", t=PACK),
+            )
 
-        def gather(c):
-            s0, n = starts[c], WIDTHS[c]
-            tile = keep.tile([P, PACK, n], F32, name="picked%d" % c, tag=PICKED[c], align_bytes=64)
-            picked.append(tile)
+        def gather(c, tag):
+            n = CHUNKS[c]
+            picked = keep.tile([P, PACK, n], F32, name="picked%d" % c, tag=tag, align_bytes=64)
             for t in range(PACK):
-                cuts = FIRST_CUTS[c] if t == 0 else [0, n]
+                cuts = (0, EARLY[c], n) if t == 0 and c < len(EARLY) else (0, n)
                 for a, b in zip(cuts[:-1], cuts[1:]):
+                    first, end = slot0[c] + a, slot0[c] + b
                     nc.vector.tensor_tensor(
-                        tile[:, t, a:b],
-                        tokens[t][:].indirect(offsets[:, (s0 + a) // 16:(s0 + b) // 16]),
-                        gates[:, s0 + a:s0 + b],
+                        picked[:, t, a:b],
+                        planes[t][:].indirect(slot_tokens[:, first // PER_COLUMN:end // PER_COLUMN]),
+                        gates[:, first:end],
                         MULT,
                     )
+            return picked
 
-        def mover(on_vector):
-            return nc.vector.tensor_copy if on_vector else nc.scalar.copy
+        def round_x(c, picked, tag):
+            rounded = keep.tile([P, CHUNKS[c] * PACK], BF16, name="x_round%d" % c, tag=tag, align_bytes=64)
+            nc.scalar.copy(
+                rounded[:].rearrange("p (j i t) -> p j t i", i=RUN, t=PACK),
+                picked[:].rearrange("p t (j i) -> p j t i", i=RUN),
+            )
+            return rounded
 
-        def round_x(c, on_vector):
-            tile = keep.tile([P, WIDTHS[c] * PACK], BF16, name="x_round%d" % c, tag=REUSE[c], align_bytes=64)
-            x_round.setdefault(c, tile)
-            mover(on_vector)(
-                x_round[c][:].rearrange("p (c i t) -> p c t i", i=2, t=PACK),
-                picked[c][:].rearrange("p t (c i) -> p c t i", i=2),
+        def round_w(g):
+            q, j = place[expert0[g]]
+            columns = w_round[q][:, j * N * PACK:(j + W_LOADS[g]) * N * PACK]
+            nc.scalar.copy(
+                columns.rearrange("p (e n i t) -> p e n t i", e=W_LOADS[g], i=RUN, t=PACK),
+                w_raw[g][:].rearrange("p e t (n i) -> p e n t i", i=RUN),
             )
 
-        def round_w(g, on_vector):
-            q, j = owner[e0[g]]
-            mover(on_vector)(
-                w_round[q][:, j * N * PACK:(j + W_GROUPS[g]) * N * PACK].rearrange("p (e c i t) -> p e c t i", e=W_GROUPS[g], i=2, t=PACK),
-                w_raw[g][:].rearrange("p e t (c i) -> p e c t i", i=2),
-            )
-
-        def quantize_x(c, j):
-            a, b = Q_CUTS[c][j], Q_CUTS[c][j + 1]
+        def quantize_x(c, rounded, a, b):
             nc.vector.quantize_mx(
                 out=x_codes[c][:, a:b].bitcast(FP8X4),
                 scales=x_scales[c][:, a:b],
-                in_=x_round[c][:, a * PACK:b * PACK],
+                in_=rounded[:, a * PACK:b * PACK],
             )
 
-        def quantize_w(g):
-            nc.vector.quantize_mx(out=w_codes[g][:].bitcast(FP8X4), scales=w_scales[g][:], in_=w_round[g][:])
+        def quantize_w(q):
+            nc.vector.quantize_mx(out=w_codes[q][:].bitcast(FP8X4), scales=w_scales[q][:], in_=w_round[q][:])
 
-        def multiply(c, piece):
-            for j in range(Q_CUTS[c][piece] // C, Q_CUTS[c][piece + 1] // C):
-                g, e = owner[starts[c] // C + j]
-                b, b0 = divmod(j * C, BANK)
-                cols = slice(j * C, (j + 1) * C)
-                outs = slice(e * N, (e + 1) * N)
+        def multiply(c, a, b):
+            for first in range(a, b, C):
+                q, j = place[(slot0[c] + first) // C]
+                bank, column = divmod(first, BANK)
+                slots = slice(first, first + C)
+                features = slice(j * N, (j + 1) * N)
                 nc.tensor.matmul_mx(
-                    out=sums[c][b][:, b0:b0 + C],
-                    lhsT=w_codes[g][:, outs].bitcast(FP8X4),
-                    lhsT_scale=w_scales[g][:, outs],
-                    rhs=x_codes[c][:, cols].bitcast(FP8X4),
-                    rhs_scale=x_scales[c][:, cols],
+                    out=banks[c][bank][:, column:column + C],
+                    lhsT=w_codes[q][:, features].bitcast(FP8X4),
+                    lhsT_scale=w_scales[q][:, features],
+                    rhs=x_codes[c][:, slots].bitcast(FP8X4),
+                    rhs_scale=x_scales[c][:, slots],
                     start=True,
                     stop=True,
                 )
 
-        def empty(c, b, on_vector):
-            bank = sums[c][b]
-            s0 = starts[c] + b * BANK
-            mover(on_vector)(y[:, s0:s0 + bank.shape[1]], bank[:])
+        def empty(c, bank, copy):
+            first = slot0[c] + bank * BANK
+            copy(y[:, first:first + banks[c][bank].shape[1]], banks[c][bank][:])
 
-        for item in STEPS:
-            kind, n = item[0], int(item[1])
-            if kind == "G":
-                gather(n)
-            if kind in "Xx":
-                round_x(n, kind == "x")
-            if kind in "Ww":
-                round_w(n, kind == "w")
-            if kind == "Q":
-                quantize_x(n, int(item[2]))
-            if kind == "R":
-                quantize_w(n)
-            if kind == "M":
-                multiply(n, int(item[2]))
-            if kind in "Ee":
-                empty(n, int(item[2]), kind == "e")
+        load_plane(0)
+        nc.sync.dma_start(slot_tokens[:], offs)
+        load_gate(0, EARLY[0])
+        load_gate(EARLY[0], slot0[1])
+        for t in range(1, PACK):
+            load_plane(t)
+        load_gate(slot0[1], slot0[1] + EARLY[1])
+        load_w(1)
+        load_gate(slot0[1] + EARLY[1], slot0[2])
+        for g in (2, 4, 0):
+            load_w(g)
+        load_gate(slot0[2], slot0[3])
+        load_w(5)
+        load_gate(slot0[3], S)
+        for g in (6, 3):
+            load_w(g)
+        for r, pos in enumerate((pos1, pos2, pos3, pos4)):
+            nc.sync.dma_start(token_slots[r][:], pos)
 
-        last = []
+        picked0 = gather(0, "picked_even")
+        picked1 = gather(1, "picked_odd")
+        round_w(1)
+        x_round0 = round_x(0, picked0, "w_raw1")
+        quantize_x(0, x_round0, 0, CHUNKS[0])
+        for g in (2, 4, 0):
+            round_w(g)
+        quantize_w(0)
+        multiply(0, 0, CHUNKS[0])
+
+        picked2 = gather(2, "picked_even")
+        x_round1 = round_x(1, picked1, "w_raw0")
+        quantize_x(1, x_round1, 0, CHUNKS[1])
+        for g, q in ((5, 2), (6, 3), (3, 1)):
+            round_w(g)
+            quantize_w(q)
+        multiply(1, 0, CHUNKS[1])
+        empty(0, 0, nc.scalar.copy)
+
+        picked3 = gather(3, "w_round1")
+        x_round2 = round_x(2, picked2, "w_raw3")
+        quantize_x(2, x_round2, 0, BANK)
+        multiply(2, 0, BANK)
+
+        picked4 = gather(4, "picked_even")
+        quantize_x(2, x_round2, BANK, CHUNKS[2])
+        multiply(2, BANK, CHUNKS[2])
+        for bank in range(2):
+            empty(1, bank, nc.scalar.copy)
+        x_round3 = round_x(3, picked3, "x_round3")
+        for a, b in ((0, 2 * C), (2 * C, CHUNKS[3])):
+            quantize_x(3, x_round3, a, b)
+            multiply(3, a, b)
+        x_round4 = round_x(4, picked4, "x_round4")
+        quantize_x(4, x_round4, 0, CHUNKS[4])
+        multiply(4, 0, CHUNKS[4])
+
+        for bank in range(2):
+            empty(2, bank, nc.scalar.copy)
+        empty(3, 0, nc.vector.tensor_copy)
+        empty(4, 0, nc.vector.tensor_copy)
+
+        totals = []
         for r in range(TOP):
-            cuts = OUT_CUTS[r]
+            cuts = LAST_CUTS if r == TOP - 1 else HALVES
             total = keep.tile([P, T], F32, name="total%d" % r)
             for a, b in zip(cuts[:-1], cuts[1:]):
-                window = y[:].indirect(back[r][:, a // 16:b // 16])
+                results = y[:].indirect(token_slots[r][:, a // PER_COLUMN:b // PER_COLUMN])
                 if r == 0:
-                    nc.vector.tensor_copy(total[:, a:b], window)
+                    nc.vector.tensor_copy(total[:, a:b], results)
                 else:
-                    nc.vector.tensor_tensor(total[:, a:b], window, last[-1][:, a:b], ADD)
+                    nc.vector.tensor_tensor(total[:, a:b], results, totals[-1][:, a:b], ADD)
                 if r == TOP - 1:
                     nc.sync.dma_start(out[:, a:b], total[:, a:b])
-            last.append(total)
+            totals.append(total)

from contextlib import ExitStack

import concourse.mybir as mybir

K, T, E, C, N = 512, 768, 24, 128, 128
TOP = 4
S = E * C

FLOPS = 2 * K * N * S
BYTES = 4 * (K * T + E * K * N + S + N * T) + 2 * 128 * (S + TOP * T) // 16

F32 = mybir.dt.float32
BF16 = mybir.dt.bfloat16
U32 = mybir.dt.uint32
U16 = mybir.dt.uint16
U8 = mybir.dt.uint8
FP8X4 = mybir.dt.float8_e4m3fn_x4
MULT = mybir.AluOpType.mult
ADD = mybir.AluOpType.add

P = 128
PACK = 4
PER_COLUMN = 16
BANK = 512
RUN = 2

CHUNKS = (512, 1024, 1024, 384, 128)
WINDOW = 1152
W_LOADS = (4, 2, 2, 4, 4, 4, 4)
W_SETS = (4, 8, 8, 4)
EARLY = (128, 512)
HALVES = (0, 384, 768)
LAST_CUTS = (0, 384, 640, 768)


def offsets_of(sizes):
    return [sum(sizes[:i]) for i in range(len(sizes))]


def tile_moe_pre_lin_none_kernel(tc, xT, w, gate, offs, pos1, pos2, pos3, pos4, out):
    nc = tc.nc
    slot0 = offsets_of(CHUNKS)
    expert0 = offsets_of(W_LOADS)
    place = [(q, j) for q, n in enumerate(W_SETS) for j in range(n)]

    with ExitStack() as ctx:
        keep = ctx.enter_context(tc.tile_pool(name="keep", bufs=1))
        psum = ctx.enter_context(tc.psum_pool(name="psum", bufs=1))

        slot_tokens = keep.tile([P, S // PER_COLUMN], U16, name="slot_tokens")
        token_slots = [keep.tile([P, T // PER_COLUMN], U16, name="token_slots%d" % r) for r in range(TOP)]
        planes = [keep.tile([P, WINDOW], F32, name="plane%d" % t) for t in range(PACK)]
        gates = keep.tile([P, S], F32, name="gates")
        w_raw = [
            keep.tile([P, n, PACK, N], F32, name="w_raw%d" % g, tag="w_raw%d" % g, align_bytes=64)
            for g, n in enumerate(W_LOADS)
        ]
        w_round = [
            keep.tile([P, n * N * PACK], BF16, name="w_round%d" % q, tag="w_round%d" % q, align_bytes=64)
            for q, n in enumerate(W_SETS)
        ]
        w_codes = [keep.tile([P, n * N], U32, name="w_codes%d" % q, align_bytes=64) for q, n in enumerate(W_SETS)]
        w_scales = [keep.tile([P, n * N], U8, name="w_scales%d" % q, align_bytes=64) for q, n in enumerate(W_SETS)]
        y = keep.tile([P, S], F32, name="y")
        x_codes = [keep.tile([P, n], U32, name="x_codes%d" % c, align_bytes=64) for c, n in enumerate(CHUNKS)]
        x_scales = [keep.tile([P, n], U8, name="x_scales%d" % c, align_bytes=64) for c, n in enumerate(CHUNKS)]
        banks = [
            [psum.tile([P, min(BANK, n - b)], F32, name="bank%d_%d" % (c, b)) for b in range(0, n, BANK)]
            for c, n in enumerate(CHUNKS)
        ]

        x_rows = xT.rearrange("(p t) j -> p t j", t=PACK)

        def load_plane(t):
            nc.sync.dma_start(planes[t][:, 0:T], x_rows[:, t, :])

        def load_gate(a, b):
            nc.sync.dma_start(gates[:, a:b], gate[0:P, a:b])

        def load_w(g):
            nc.sync.dma_start(
                w_raw[g][:].rearrange("p e t n -> p e (t n)"),
                w[expert0[g]:expert0[g] + W_LOADS[g]].rearrange("e (p t) n -> p e (t n)", t=PACK),
            )

        def gather(c, tag):
            n = CHUNKS[c]
            picked = keep.tile([P, PACK, n], F32, name="picked%d" % c, tag=tag, align_bytes=64)
            for t in range(PACK):
                cuts = (0, EARLY[c], n) if t == 0 and c < len(EARLY) else (0, n)
                for a, b in zip(cuts[:-1], cuts[1:]):
                    first, end = slot0[c] + a, slot0[c] + b
                    nc.vector.tensor_tensor(
                        picked[:, t, a:b],
                        planes[t][:].indirect(slot_tokens[:, first // PER_COLUMN:end // PER_COLUMN]),
                        gates[:, first:end],
                        MULT,
                    )
            return picked

        def round_x(c, picked, tag):
            rounded = keep.tile([P, CHUNKS[c] * PACK], BF16, name="x_round%d" % c, tag=tag, align_bytes=64)
            nc.scalar.copy(
                rounded[:].rearrange("p (j i t) -> p j t i", i=RUN, t=PACK),
                picked[:].rearrange("p t (j i) -> p j t i", i=RUN),
            )
            return rounded

        def round_w(g):
            q, j = place[expert0[g]]
            columns = w_round[q][:, j * N * PACK:(j + W_LOADS[g]) * N * PACK]
            nc.scalar.copy(
                columns.rearrange("p (e n i t) -> p e n t i", e=W_LOADS[g], i=RUN, t=PACK),
                w_raw[g][:].rearrange("p e t (n i) -> p e n t i", i=RUN),
            )

        def quantize_x(c, rounded, a, b):
            nc.vector.quantize_mx(
                out=x_codes[c][:, a:b].bitcast(FP8X4),
                scales=x_scales[c][:, a:b],
                in_=rounded[:, a * PACK:b * PACK],
            )

        def quantize_w(q):
            nc.vector.quantize_mx(out=w_codes[q][:].bitcast(FP8X4), scales=w_scales[q][:], in_=w_round[q][:])

        def multiply(c, a, b):
            for first in range(a, b, C):
                q, j = place[(slot0[c] + first) // C]
                bank, column = divmod(first, BANK)
                slots = slice(first, first + C)
                features = slice(j * N, (j + 1) * N)
                nc.tensor.matmul_mx(
                    out=banks[c][bank][:, column:column + C],
                    lhsT=w_codes[q][:, features].bitcast(FP8X4),
                    lhsT_scale=w_scales[q][:, features],
                    rhs=x_codes[c][:, slots].bitcast(FP8X4),
                    rhs_scale=x_scales[c][:, slots],
                    start=True,
                    stop=True,
                )

        def empty(c, bank, copy):
            first = slot0[c] + bank * BANK
            copy(y[:, first:first + banks[c][bank].shape[1]], banks[c][bank][:])

        load_plane(0)
        nc.sync.dma_start(slot_tokens[:], offs)
        load_gate(0, EARLY[0])
        load_gate(EARLY[0], slot0[1])
        for t in range(1, PACK):
            load_plane(t)
        load_gate(slot0[1], slot0[1] + EARLY[1])
        load_w(1)
        load_gate(slot0[1] + EARLY[1], slot0[2])
        for g in (2, 4, 0):
            load_w(g)
        load_gate(slot0[2], slot0[3])
        load_w(5)
        load_gate(slot0[3], S)
        for g in (6, 3):
            load_w(g)
        for r, pos in enumerate((pos1, pos2, pos3, pos4)):
            nc.sync.dma_start(token_slots[r][:], pos)

        picked0 = gather(0, "picked_even")
        picked1 = gather(1, "picked_odd")
        round_w(1)
        x_round0 = round_x(0, picked0, "w_raw1")
        quantize_x(0, x_round0, 0, CHUNKS[0])
        for g in (2, 4, 0):
            round_w(g)
        quantize_w(0)
        multiply(0, 0, CHUNKS[0])

        picked2 = gather(2, "picked_even")
        x_round1 = round_x(1, picked1, "w_raw0")
        quantize_x(1, x_round1, 0, CHUNKS[1])
        for g, q in ((5, 2), (6, 3), (3, 1)):
            round_w(g)
            quantize_w(q)
        multiply(1, 0, CHUNKS[1])
        empty(0, 0, nc.scalar.copy)

        picked3 = gather(3, "w_round1")
        x_round2 = round_x(2, picked2, "w_raw3")
        quantize_x(2, x_round2, 0, BANK)
        multiply(2, 0, BANK)

        picked4 = gather(4, "picked_even")
        quantize_x(2, x_round2, BANK, CHUNKS[2])
        multiply(2, BANK, CHUNKS[2])
        for bank in range(2):
            empty(1, bank, nc.scalar.copy)
        x_round3 = round_x(3, picked3, "x_round3")
        for a, b in ((0, 2 * C), (2 * C, CHUNKS[3])):
            quantize_x(3, x_round3, a, b)
            multiply(3, a, b)
        x_round4 = round_x(4, picked4, "x_round4")
        quantize_x(4, x_round4, 0, CHUNKS[4])
        multiply(4, 0, CHUNKS[4])

        for bank in range(2):
            empty(2, bank, nc.scalar.copy)
        empty(3, 0, nc.vector.tensor_copy)
        empty(4, 0, nc.vector.tensor_copy)

        totals = []
        for r in range(TOP):
            cuts = LAST_CUTS if r == TOP - 1 else HALVES
            total = keep.tile([P, T], F32, name="total%d" % r)
            for a, b in zip(cuts[:-1], cuts[1:]):
                results = y[:].indirect(token_slots[r][:, a // PER_COLUMN:b // PER_COLUMN])
                if r == 0:
                    nc.vector.tensor_copy(total[:, a:b], results)
                else:
                    nc.vector.tensor_tensor(total[:, a:b], results, totals[-1][:, a:b], ADD)
                if r == TOP - 1:
                    nc.sync.dma_start(out[:, a:b], total[:, a:b])
            totals.append(total)
